import numpy as np
import ml_dtypes


def mxq(x, axis, fmt="e4m3"):
    dtype, down = {"e4m3": (ml_dtypes.float8_e4m3fn, 7), "e5m2": (ml_dtypes.float8_e5m2, 14)}[fmt]
    v = np.moveaxis(np.asarray(x, np.float32).astype(ml_dtypes.bfloat16).astype(np.float64), axis, -1)
    blocks = v.reshape(v.shape[:-1] + (-1, 32))
    amax = np.abs(blocks).max(-1, keepdims=True)
    byte = np.maximum(np.where(amax > 0, np.frexp(amax)[1] - 1 + 127, 0) - down, 1)
    scale = np.exp2(byte - 127.0)
    codes = (blocks / scale).astype(np.float32).astype(dtype).astype(np.float64)
    return np.moveaxis((codes * scale).reshape(v.shape), -1, axis)


WIDE = False


def mx_kscale(k):
    if not WIDE:
        return np.ones(k)
    levels = np.array([10, -10, 5, -5, 0])
    if k % 512:
        return np.exp2(np.random.permutation(np.resize(levels, k // 32))).repeat(32)
    a = np.empty((k // 512, 16))
    for p in range(k // 512):
        a[p, :8] = np.random.permutation(np.resize(levels, 8))
        for g in range(8):
            far = levels[np.abs(levels - a[p, g]) >= 10]
            a[p, g + 8] = far[np.random.randint(len(far))]
    return np.exp2(a.ravel()).repeat(32)


def f64(x):
    return np.asarray(x).astype(np.float64)


def striped(idx):
    return np.tile(np.asarray(idx).reshape(-1, 16).T, (8, 1)).astype(np.uint16)


def unstriped(offs):
    return offs[:16].T.reshape(-1).astype(np.int64)


def striped8(idx):
    return np.asarray(idx).reshape(8, -1, 16).transpose(0, 2, 1).reshape(128, -1).astype(np.uint16)


def unstriped8(offs):
    return offs.reshape(8, 16, -1).transpose(0, 2, 1).reshape(8, -1).astype(np.int64)


def pick8(x, idx, run):
    r = np.arange(len(x))
    return x[r[:, None], idx[r % (8 * run) // run]]


E2M1 = np.array([0.0, 0.5, 1.0, 1.5, 2.0, 3.0, 4.0, 6.0, -0.0, -0.5, -1.0, -1.5, -2.0, -3.0, -4.0, -6.0])


def pack_weight(w, fmt):
    k, n = w.shape
    w = f64(np.asarray(w, np.float32).astype(ml_dtypes.bfloat16)).reshape(k // 32, 32, n)
    amax = np.abs(w).max(1)
    if fmt == "e4m3":
        byte = np.frexp(amax)[1] - 1 + 127 - 7
    else:
        mant, ex = np.frexp(amax / 6.0)
        byte = np.where(mant > 0.5, ex, ex - 1) + 127
    byte = np.clip(np.where(amax > 0, byte, 1), 1, 254)
    scaled = (w * np.exp2(127.0 - byte)[:, None, :]).reshape(k, n).astype(np.float32)
    by_word = np.ascontiguousarray(scaled.reshape(k // 512, 128, 4, n).transpose(0, 1, 3, 2))
    if fmt == "e4m3":
        words = by_word.astype(ml_dtypes.float8_e4m3fn).view(np.uint8)
    else:
        c = by_word.astype(ml_dtypes.float4_e2m1fn).view(np.uint8) & 0xF
        words = (c[..., 0::2] | (c[..., 1::2] << 4)).reshape(k // 512, 128, 2 * n)
    return np.ascontiguousarray(words), np.ascontiguousarray(byte.astype(np.uint8).reshape(k // 512, 16, n))


def unpack_weight(words, scales, fmt):
    g, _, n = scales.shape
    words = np.ascontiguousarray(words).reshape(g, 128, n, -1)
    if fmt == "e4m3":
        vals = words.view(ml_dtypes.float8_e4m3fn).astype(np.float64)
    else:
        nib = np.empty((g, 128, n, 4), np.uint8)
        nib[..., 0::2] = words & 0xF
        nib[..., 1::2] = words >> 4
        vals = E2M1[nib]
    vals = vals * np.repeat(np.exp2(scales.astype(np.float64) - 127.0), 8, axis=1)[..., None]
    return vals.transpose(0, 1, 3, 2).reshape(g * 512, n)


def sigmoid(v):
    return 1.0 / (1.0 + np.exp(-v))


K, R, F, T, J, M = 512, 128, 512, 2048, 512, 256


def setup_inputs():
    n = np.random.standard_normal
    idx = np.random.permutation(T)[:J]
    idx2 = np.stack([np.random.permutation(J)[:M] for _ in range(8)])
    idx3 = np.stack([np.random.permutation(J)[:M] for _ in range(8)])
    fk = mx_kscale(K)
    ff = mx_kscale(F)
    tabp = pack_weight(n((K, T)) / fk[:, None], "e4m3")
    return {
        "tab_words": tabp[0],
        "tab_scales": tabp[1],
        "w1": (n((K, R)) * 1 / np.sqrt(K) * fk[:, None]).astype(np.float32),
        "gain": (np.random.uniform(0.5, 1.5, (R, 1))).astype(np.float32),
        "steep": (np.random.uniform(0.7, 2.5, (R, 1))).astype(np.float32),
        "wo": (n((F, R)) * 1 / np.sqrt(F) * ff[:, None]).astype(np.float32),
        "dy": (n((F, M)) / ff[:, None]).astype(np.float32),
        "old": (0.5 * n((R, J))).astype(np.float32),
        "offs": striped(idx),
        "offs2": striped8(idx2),
        "offs3": striped8(idx3),
    }


def reference(tab_words, tab_scales, w1, gain, steep, wo, dy, old, offs, offs2, offs3):
    idx = unstriped(offs)
    idx2 = unstriped8(offs2)
    idx3 = unstriped8(offs3)
    tabu = unpack_weight(tab_words, tab_scales, "e4m3")
    w1q = mxq(f64(w1), 0, "e4m3")
    tabidxg = tabu[:, idx]
    a = w1q.T @ tabidxg
    h1 = a * f64(gain)
    gt = sigmoid((pick8(h1, idx2, 16) - pick8(h1, idx3, 16)) * f64(steep))
    woq = mxq(f64(wo), 0, "e4m3")
    dyq = mxq(f64(dy), 0, "e4m3")
    c0 = woq.T @ dyq
    dgt = c0 * (pick8(h1, idx2, 16) - pick8(h1, idx3, 16))
    s1 = np.zeros((R, J))
    s1[np.arange(R)[:, None], idx3[np.arange(R) % 128 // 16]] = c0
    e2 = c0 * gt * (-1.0)
    s2 = np.zeros((R, J))
    s2[np.arange(R)[:, None], idx3[np.arange(R) % 128 // 16]] = e2
    e3 = dgt * gt * (1.0 - gt) * f64(steep) * (-1.0)
    s3 = np.zeros((R, J))
    s3[np.arange(R)[:, None], idx3[np.arange(R) % 128 // 16]] = e3
    e4 = c0 * gt
    s4 = np.zeros((R, J))
    s4[np.arange(R)[:, None], idx2[np.arange(R) % 128 // 16]] = e4
    e5 = dgt * gt * (1.0 - gt) * f64(steep)
    s5 = np.zeros((R, J))
    s5[np.arange(R)[:, None], idx2[np.arange(R) % 128 // 16]] = e5
    dh1 = s1 + s2 + s3 + s4 + s5
    da = dh1 * f64(gain)
    y = da + f64(old)
    return y

@@ -1,0 +1,182 @@
+from contextlib import ExitStack
+
+import concourse.mybir as mybir
+
+K, R, F, T, J, M = 512, 128, 512, 2048, 512, 256
+FLOPS = 2 * K * R * J + 2 * F * R * M
+
+F32 = mybir.dt.float32
+BF16 = mybir.dt.bfloat16
+I32 = mybir.dt.int32
+U32 = mybir.dt.uint32
+U16 = mybir.dt.uint16
+U8 = mybir.dt.uint8
+FP8X4 = mybir.dt.float8_e4m3fn_x4
+ALU = mybir.AluOpType
+ACT = mybir.ActivationFunctionType
+
+P = 128
+PACK = 4
+GROUP = 16
+SLOT_PIECES = (256, 128, 128)
+HALF = M // 2
+
+
+def rows_by_four(x):
+    return x.rearrange("(p t) w -> p t w", t=PACK)
+
+
+def weave_out(grouped):
+    return grouped[:].rearrange("p (c i) t -> p c t i", i=PACK)
+
+
+def weave_in(raw):
+    return raw[:].rearrange("p t (c i) -> p c t i", i=PACK)
+
+
+def quantize(nc, pool, grouped, name):
+    width = grouped.shape[1]
+    codes = pool.tile([P, width], U32, name=name + "_codes", align_bytes=64)
+    scales = pool.tile([P, width], U8, name=name + "_scales", align_bytes=64)
+    nc.vector.quantize_mx(
+        out=codes[:].bitcast(FP8X4),
+        scales=scales[:],
+        in_=grouped[:].rearrange("p w t -> p (w t)"),
+    )
+    return codes, scales
+
+
+def tile_attend_csoftlarger_kernel(tc, tab_words, tab_scales, w1, gain, steep, wo, dy, old, offs, offs2, offs3, out):
+    nc = tc.nc
+    with ExitStack() as ctx:
+        sb = ctx.enter_context(tc.tile_pool(name="sb", bufs=1))
+        ps = ctx.enter_context(tc.psum_pool(name="ps", bufs=1))
+
+        slots = sb.tile([P, J // GROUP], U16, name="slots")
+        picks2 = sb.tile([P, M // GROUP], U16, name="picks2")
+        picks3 = sb.tile([P, M // GROUP], U16, name="picks3")
+        words = sb.tile([P, T], U32, name="words")
+        plane = sb.tile([P, T], U8, name="plane")
+        w1_raw = sb.tile([P, PACK, R], F32, name="w1_raw")
+        wo_raw = sb.tile([P, PACK, R], F32, name="wo_raw")
+        dy_raw = sb.tile([P, PACK, M], F32, name="dy_raw")
+        old_sb = sb.tile([P, J], F32, name="old_sb")
+        gain_sb = sb.tile([P, 1], F32, name="gain_sb")
+        steep_sb = sb.tile([P, 1], F32, name="steep_sb")
+
+        nc.vector.memset(plane[:].bitcast(I32), 0)
+        for q in range(4):
+            nc.scalar.dma_start(
+                out=plane[32 * q : 32 * q + 4, :].bitcast(I32),
+                in_=tab_scales[0][4 * q : 4 * q + 4, :].bitcast(I32),
+            )
+        nc.sync.dma_start(slots[:], offs)
+        nc.sync.dma_start(out=w1_raw[:], in_=rows_by_four(w1))
+        nc.sync.dma_start(
+            out=words[:].bitcast(I32),
+            in_=tab_words[0].rearrange("p n t -> p (n t)").bitcast(I32),
+        )
+        nc.gpsimd.dma_start(out=gain_sb[:], in_=gain)
+        nc.gpsimd.dma_start(out=steep_sb[:], in_=steep)
+        nc.sync.dma_start(out=dy_raw[:], in_=rows_by_four(dy))
+        nc.sync.dma_start(out=wo_raw[:], in_=rows_by_four(wo))
+        nc.sync.dma_start(picks3[:], offs3)
+        nc.sync.dma_start(picks2[:], offs2)
+        nc.sync.dma_start(out=old_sb[:], in_=old)
+
+        placed2 = sb.tile([P, J], F32, name="placed2")
+        placed3 = sb.tile([P, J], F32, name="placed3")
+        nc.vector.memset(placed2[:], 0.0)
+        nc.vector.memset(placed3[:], 0.0)
+
+        w1_grouped = sb.tile([P, R, PACK], BF16, name="w1_grouped", align_bytes=64)
+        nc.scalar.activation(out=weave_out(w1_grouped), in_=weave_in(w1_raw), func=ACT.Copy)
+        w1_codes, w1_scales = quantize(nc, sb, w1_grouped, "w1")
+
+        half_steep = sb.tile([P, 1], F32, name="half_steep")
+        nc.vector.tensor_scalar(half_steep[:], steep_sb[:], 0.5, None, ALU.mult)
+        neg_half_gain = sb.tile([P, 1], F32, name="neg_half_gain")
+        nc.vector.tensor_scalar(neg_half_gain[:], gain_sb[:], -0.5, None, ALU.mult)
+
+        tab_bytes = sb.tile([P, J], U8, name="tab_bytes", align_bytes=64)
+        nc.vector.tensor_copy(tab_bytes[:], plane[:].indirect(slots[:]))
+
+        h1 = sb.tile([P, J], F32, name="h1")
+        j0 = 0
+        for i, n in enumerate(SLOT_PIECES):
+            tab_codes = sb.tile([P, n], U32, name="tab_codes%d" % i, align_bytes=64)
+            nc.vector.tensor_copy(tab_codes[:], words[:].indirect(slots[:, j0 // GROUP : (j0 + n) // GROUP]))
+            a = ps.tile([P, n], F32, name="a%d" % i)
+            nc.tensor.matmul_mx(
+                out=a[:],
+                lhsT=w1_codes[:].bitcast(FP8X4),
+                lhsT_scale=w1_scales[:],
+                rhs=tab_codes[:].bitcast(FP8X4),
+                rhs_scale=tab_bytes[:, j0 : j0 + n],
+                start=True,
+                stop=True,
+            )
+            nc.scalar.activation(out=h1[:, j0 : j0 + n], in_=a[:], func=ACT.Copy, scale=gain_sb[:])
+            j0 = j0 + n
+
+        dy_grouped = sb.tile([P, M, PACK], BF16, name="dy_grouped", align_bytes=64)
+        nc.vector.tensor_copy(weave_out(dy_grouped), weave_in(dy_raw))
+
+        halves = [slice(h * HALF, (h + 1) * HALF) for h in range(2)]
+        lists2 = [picks2[:, h * HALF // GROUP : (h + 1) * HALF // GROUP] for h in range(2)]
+        lists3 = [picks3[:, h * HALF // GROUP : (h + 1) * HALF // GROUP] for h in range(2)]
+
+        def halves_tile(name):
+            return [sb.tile([P, HALF], F32, name="%s%d" % (name, h)) for h in range(2)]
+
+        pick3 = halves_tile("pick3")
+        nc.vector.tensor_copy(pick3[0][:], h1[:].indirect(lists3[0]))
+        nc.scalar.activation(out=pick3[1][:], in_=h1[:].indirect(lists3[1]), func=ACT.Copy)
+        diff = halves_tile("diff")
+        th = halves_tile("th")
+        for h in range(2):
+            nc.vector.tensor_tensor(diff[h][:], h1[:].indirect(lists2[h]), pick3[h][:], ALU.subtract)
+            nc.scalar.activation(out=th[h][:], in_=diff[h][:], func=ACT.Tanh, scale=half_steep[:])
+
+        wo_grouped = sb.tile([P, R, PACK], BF16, name="wo_grouped", align_bytes=64)
+        nc.vector.tensor_copy(weave_out(wo_grouped), weave_in(wo_raw))
+        dy_codes, dy_scales = quantize(nc, sb, dy_grouped, "dy")
+        wo_codes, wo_scales = quantize(nc, sb, wo_grouped, "wo")
+        c0 = ps.tile([P, M], F32, name="c0")
+        nc.tensor.matmul_mx(
+            out=c0[:],
+            lhsT=wo_codes[:].bitcast(FP8X4),
+            lhsT_scale=wo_scales[:],
+            rhs=dy_codes[:].bitcast(FP8X4),
+            rhs_scale=dy_scales[:],
+            start=True,
+            stop=True,
+        )
+
+        hz = halves_tile("hz")
+        th_plus = halves_tile("th_plus")
+        bend = halves_tile("bend")
+        share2 = halves_tile("share2")
+        share3 = halves_tile("share3")
+        for h in range(2):
+            nc.vector.tensor_scalar(hz[h][:], diff[h][:], half_steep[:], None, ALU.mult)
+            nc.scalar.activation(out=th_plus[h][:], in_=th[h][:], func=ACT.Copy, bias=1.0)
+        grad = sb.tile([P, M], F32, name="grad")
+        nc.scalar.activation(out=grad[:], in_=c0[:], func=ACT.Copy, scale=neg_half_gain[:])
+        for h in range(2):
+            nc.vector.scalar_tensor_tensor(bend[h][:], th[h][:], 1.0, hz[h][:], ALU.subtract, ALU.mult)
+        for h in range(2):
+            nc.vector.scalar_tensor_tensor(share2[h][:], bend[h][:], 1.0, th_plus[h][:], ALU.subtract, ALU.mult)
+            nc.scalar.activation(out=share3[h][:], in_=share2[h][:], func=ACT.Copy, scale=-1.0, bias=-2.0)
+        for h in range(2):
+            nc.vector.tensor_tensor(placed2[:].indirect(lists2[h]), grad[:, halves[h]], share2[h][:], ALU.mult)
+        partial = sb.tile([P, J], F32, name="partial")
+        for h in range(2):
+            nc.vector.tensor_tensor(placed3[:].indirect(lists3[h]), grad[:, halves[h]], share3[h][:], ALU.mult)
+        nc.vector.tensor_tensor(partial[:], placed2[:], old_sb[:], ALU.add)
+        for h in range(2):
+            cols = slice(h * J // 2, (h + 1) * J // 2)
+            result = sb.tile([P, J // 2], F32, name="result%d" % h)
+            nc.vector.tensor_tensor(result[:], placed3[:, cols], partial[:, cols], ALU.add)
+            queue = nc.sync if h == 0 else nc.scalar
+            queue.dma_start(out=out[:, cols], in_=result[:])

@@ -64,22 +64,23 @@ def tile_attend_csoftlarger_kernel(tc, tab_words, tab_scales, w1, gain, steep, w
         gain_sb = sb.tile([P, 1], F32, name="gain_sb")
         steep_sb = sb.tile([P, 1], F32, name="steep_sb")
 
-        nc.vector.memset(plane[:].bitcast(I32), 0)
+        nc.vector.memset(plane[:, : T // 2].bitcast(I32), 0)
+        nc.gpsimd.memset(plane[:, T // 2 :].bitcast(I32), 0)
+        nc.sync.dma_start(slots[:], offs)
+        nc.sync.dma_start(out=w1_raw[:], in_=rows_by_four(w1))
+        nc.sync.dma_start(out=wo_raw[:], in_=rows_by_four(wo))
         for q in range(4):
-            nc.scalar.dma_start(
+            nc.sync.dma_start(
                 out=plane[32 * q : 32 * q + 4, :].bitcast(I32),
                 in_=tab_scales[0][4 * q : 4 * q + 4, :].bitcast(I32),
             )
-        nc.sync.dma_start(slots[:], offs)
-        nc.sync.dma_start(out=w1_raw[:], in_=rows_by_four(w1))
         nc.sync.dma_start(
             out=words[:].bitcast(I32),
             in_=tab_words[0].rearrange("p n t -> p (n t)").bitcast(I32),
         )
-        nc.gpsimd.dma_start(out=gain_sb[:], in_=gain)
-        nc.gpsimd.dma_start(out=steep_sb[:], in_=steep)
+        nc.sync.dma_start(out=gain_sb[:], in_=gain)
         nc.sync.dma_start(out=dy_raw[:], in_=rows_by_four(dy))
-        nc.sync.dma_start(out=wo_raw[:], in_=rows_by_four(wo))
+        nc.sync.dma_start(out=steep_sb[:], in_=steep)
         nc.sync.dma_start(picks3[:], offs3)
         nc.sync.dma_start(picks2[:], offs2)
         nc.sync.dma_start(out=old_sb[:], in_=old)
@@ -91,15 +92,18 @@ def tile_attend_csoftlarger_kernel(tc, tab_words, tab_scales, w1, gain, steep, w
 
         w1_grouped = sb.tile([P, R, PACK], BF16, name="w1_grouped", align_bytes=64)
         nc.scalar.activation(out=weave_out(w1_grouped), in_=weave_in(w1_raw), func=ACT.Copy)
-        w1_codes, w1_scales = quantize(nc, sb, w1_grouped, "w1")
-
-        half_steep = sb.tile([P, 1], F32, name="half_steep")
-        nc.vector.tensor_scalar(half_steep[:], steep_sb[:], 0.5, None, ALU.mult)
-        neg_half_gain = sb.tile([P, 1], F32, name="neg_half_gain")
-        nc.vector.tensor_scalar(neg_half_gain[:], gain_sb[:], -0.5, None, ALU.mult)
+        wo_grouped = sb.tile([P, R, PACK], BF16, name="wo_grouped", align_bytes=64)
+        nc.scalar.activation(out=weave_out(wo_grouped), in_=weave_in(wo_raw), func=ACT.Copy)
 
         tab_bytes = sb.tile([P, J], U8, name="tab_bytes", align_bytes=64)
         nc.vector.tensor_copy(tab_bytes[:], plane[:].indirect(slots[:]))
+        w1_codes, w1_scales = quantize(nc, sb, w1_grouped, "w1")
+        wo_codes, wo_scales = quantize(nc, sb, wo_grouped, "wo")
+
+        half_steep = sb.tile([P, 1], F32, name="half_steep")
+        nc.gpsimd.tensor_scalar(half_steep[:], steep_sb[:], 0.5, 0.0, ALU.mult, ALU.add)
+        neg_half_gain = sb.tile([P, 1], F32, name="neg_half_gain")
+        nc.gpsimd.tensor_scalar(neg_half_gain[:], gain_sb[:], -0.5, 0.0, ALU.mult, ALU.add)
 
         h1 = sb.tile([P, J], F32, name="h1")
         j0 = 0
@@ -121,27 +125,7 @@ def tile_attend_csoftlarger_kernel(tc, tab_words, tab_scales, w1, gain, steep, w
 
         dy_grouped = sb.tile([P, M, PACK], BF16, name="dy_grouped", align_bytes=64)
         nc.vector.tensor_copy(weave_out(dy_grouped), weave_in(dy_raw))
-
-        halves = [slice(h * HALF, (h + 1) * HALF) for h in range(2)]
-        lists2 = [picks2[:, h * HALF // GROUP : (h + 1) * HALF // GROUP] for h in range(2)]
-        lists3 = [picks3[:, h * HALF // GROUP : (h + 1) * HALF // GROUP] for h in range(2)]
-
-        def halves_tile(name):
-            return [sb.tile([P, HALF], F32, name="%s%d" % (name, h)) for h in range(2)]
-
-        pick3 = halves_tile("pick3")
-        nc.vector.tensor_copy(pick3[0][:], h1[:].indirect(lists3[0]))
-        nc.scalar.activation(out=pick3[1][:], in_=h1[:].indirect(lists3[1]), func=ACT.Copy)
-        diff = halves_tile("diff")
-        th = halves_tile("th")
-        for h in range(2):
-            nc.vector.tensor_tensor(diff[h][:], h1[:].indirect(lists2[h]), pick3[h][:], ALU.subtract)
-            nc.scalar.activation(out=th[h][:], in_=diff[h][:], func=ACT.Tanh, scale=half_steep[:])
-
-        wo_grouped = sb.tile([P, R, PACK], BF16, name="wo_grouped", align_bytes=64)
-        nc.vector.tensor_copy(weave_out(wo_grouped), weave_in(wo_raw))
         dy_codes, dy_scales = quantize(nc, sb, dy_grouped, "dy")
-        wo_codes, wo_scales = quantize(nc, sb, wo_grouped, "wo")
         c0 = ps.tile([P, M], F32, name="c0")
         nc.tensor.matmul_mx(
             out=c0[:],
@@ -153,15 +137,33 @@ def tile_attend_csoftlarger_kernel(tc, tab_words, tab_scales, w1, gain, steep, w
             stop=True,
         )
 
+        halves = [slice(h * HALF, (h + 1) * HALF) for h in range(2)]
+        lists2 = [picks2[:, h * HALF // GROUP : (h + 1) * HALF // GROUP] for h in range(2)]
+        lists3 = [picks3[:, h * HALF // GROUP : (h + 1) * HALF // GROUP] for h in range(2)]
+
+        def halves_tile(name):
+            return [sb.tile([P, HALF], F32, name="%s%d" % (name, h)) for h in range(2)]
+
+        pick2 = sb.tile([P, M], F32, name="pick2", tag="pick2")
+        pick3 = halves_tile("pick3")
+        diff = halves_tile("diff")
+        th = halves_tile("th")
         hz = halves_tile("hz")
         th_plus = halves_tile("th_plus")
         bend = halves_tile("bend")
         share2 = halves_tile("share2")
         share3 = halves_tile("share3")
+
+        nc.vector.tensor_copy(pick2[:], h1[:].indirect(picks2[:]))
+        for h in range(2):
+            nc.scalar.activation(out=pick3[h][:], in_=h1[:].indirect(lists3[h]), func=ACT.Copy)
+        for h in range(2):
+            nc.vector.tensor_tensor(diff[h][:], pick2[:, halves[h]], pick3[h][:], ALU.subtract)
+            nc.scalar.activation(out=th[h][:], in_=diff[h][:], func=ACT.Tanh, scale=half_steep[:])
+            nc.scalar.activation(out=th_plus[h][:], in_=th[h][:], func=ACT.Copy, bias=1.0)
         for h in range(2):
             nc.vector.tensor_scalar(hz[h][:], diff[h][:], half_steep[:], None, ALU.mult)
-            nc.scalar.activation(out=th_plus[h][:], in_=th[h][:], func=ACT.Copy, bias=1.0)
-        grad = sb.tile([P, M], F32, name="grad")
+        grad = sb.tile([P, M], F32, name="grad", tag="pick2")
         nc.scalar.activation(out=grad[:], in_=c0[:], func=ACT.Copy, scale=neg_half_gain[:])
         for h in range(2):
             nc.vector.scalar_tensor_tensor(bend[h][:], th[h][:], 1.0, hz[h][:], ALU.subtract, ALU.mult)
@@ -170,13 +172,13 @@ def tile_attend_csoftlarger_kernel(tc, tab_words, tab_scales, w1, gain, steep, w
             nc.scalar.activation(out=share3[h][:], in_=share2[h][:], func=ACT.Copy, scale=-1.0, bias=-2.0)
         for h in range(2):
             nc.vector.tensor_tensor(placed2[:].indirect(lists2[h]), grad[:, halves[h]], share2[h][:], ALU.mult)
-        partial = sb.tile([P, J], F32, name="partial")
-        for h in range(2):
             nc.vector.tensor_tensor(placed3[:].indirect(lists3[h]), grad[:, halves[h]], share3[h][:], ALU.mult)
-        nc.vector.tensor_tensor(partial[:], placed2[:], old_sb[:], ALU.add)
+
+        columns = [slice(h * J // 2, (h + 1) * J // 2) for h in range(2)]
+        partial = [sb.tile([P, J // 2], F32, name="partial%d" % h) for h in range(2)]
         for h in range(2):
-            cols = slice(h * J // 2, (h + 1) * J // 2)
+            nc.vector.tensor_tensor(partial[h][:], placed2[:, columns[h]], old_sb[:, columns[h]], ALU.add)
+        for h in range(2):
             result = sb.tile([P, J // 2], F32, name="result%d" % h)
-            nc.vector.tensor_tensor(result[:], placed3[:, cols], partial[:, cols], ALU.add)
-            queue = nc.sync if h == 0 else nc.scalar
-            queue.dma_start(out=out[:, cols], in_=result[:])
+            nc.vector.tensor_tensor(result[:], placed3[:, columns[h]], partial[h][:], ALU.add)
+            (nc.sync, nc.scalar)[h].dma_start(out=out[:, columns[h]], in_=result[:])

@@ -151,8 +151,7 @@ def tile_attend_csoftlarger_kernel(tc, tab_words, tab_scales, w1, gain, steep, w
         hz = halves_tile("hz")
         th_plus = halves_tile("th_plus")
         bend = halves_tile("bend")
-        share2 = halves_tile("share2")
-        share3 = halves_tile("share3")
+        share = sb.tile([P, M], F32, name="share")
 
         nc.vector.tensor_copy(pick2[:], h1[:].indirect(picks2[:]))
         for h in range(2):
@@ -168,17 +167,18 @@ def tile_attend_csoftlarger_kernel(tc, tab_words, tab_scales, w1, gain, steep, w
         for h in range(2):
             nc.vector.scalar_tensor_tensor(bend[h][:], th[h][:], 1.0, hz[h][:], ALU.subtract, ALU.mult)
         for h in range(2):
-            nc.vector.scalar_tensor_tensor(share2[h][:], bend[h][:], 1.0, th_plus[h][:], ALU.subtract, ALU.mult)
-            nc.scalar.activation(out=share3[h][:], in_=share2[h][:], func=ACT.Copy, scale=-1.0, bias=-2.0)
-        for h in range(2):
-            nc.vector.tensor_tensor(placed2[:].indirect(lists2[h]), grad[:, halves[h]], share2[h][:], ALU.mult)
-            nc.vector.tensor_tensor(placed3[:].indirect(lists3[h]), grad[:, halves[h]], share3[h][:], ALU.mult)
+            nc.vector.scalar_tensor_tensor(share[:, halves[h]], bend[h][:], 1.0, th_plus[h][:], ALU.subtract, ALU.mult)
+        neg_sent3 = sb.tile([P, M], F32, name="neg_sent3")
+        nc.vector.tensor_tensor(placed2[:].indirect(lists2[0]), grad[:, halves[0]], share[:, halves[0]], ALU.mult)
+        nc.vector.scalar_tensor_tensor(neg_sent3[:], share[:], 2.0, grad[:], ALU.add, ALU.mult)
+        nc.vector.tensor_tensor(placed2[:].indirect(lists2[1]), grad[:, halves[1]], share[:, halves[1]], ALU.mult)
+        nc.vector.tensor_copy(placed3[:].indirect(picks3[:]), neg_sent3[:])
 
         columns = [slice(h * J // 2, (h + 1) * J // 2) for h in range(2)]
         partial = [sb.tile([P, J // 2], F32, name="partial%d" % h) for h in range(2)]
         for h in range(2):
-            nc.vector.tensor_tensor(partial[h][:], placed2[:, columns[h]], old_sb[:, columns[h]], ALU.add)
+            nc.gpsimd.tensor_tensor(partial[h][:], placed2[:, columns[h]], old_sb[:, columns[h]], ALU.add)
         for h in range(2):
             result = sb.tile([P, J // 2], F32, name="result%d" % h)
-            nc.vector.tensor_tensor(result[:], placed3[:, columns[h]], partial[h][:], ALU.add)
+            nc.vector.tensor_tensor(result[:], partial[h][:], placed3[:, columns[h]], ALU.subtract)
             (nc.sync, nc.scalar)[h].dma_start(out=out[:, columns[h]], in_=result[:])

@@ -58,7 +58,7 @@ def tile_attend_csoftlarger_kernel(tc, tab_words, tab_scales, w1, gain, steep, w
         words = sb.tile([P, T], U32, name="words")
         plane = sb.tile([P, T], U8, name="plane")
         w1_raw = sb.tile([P, PACK, R], F32, name="w1_raw")
-        wo_raw = sb.tile([P, PACK, R], F32, name="wo_raw")
+        wo_raw = sb.tile([P, PACK, R], F32, name="wo_raw", tag="wo_raw")
         dy_raw = sb.tile([P, PACK, M], F32, name="dy_raw")
         old_sb = sb.tile([P, J], F32, name="old_sb")
         gain_sb = sb.tile([P, 1], F32, name="gain_sb")
@@ -68,9 +68,8 @@ def tile_attend_csoftlarger_kernel(tc, tab_words, tab_scales, w1, gain, steep, w
         nc.gpsimd.memset(plane[:, T // 2 :].bitcast(I32), 0)
         nc.sync.dma_start(slots[:], offs)
         nc.sync.dma_start(out=w1_raw[:], in_=rows_by_four(w1))
-        nc.sync.dma_start(out=wo_raw[:], in_=rows_by_four(wo))
         for q in range(4):
-            nc.sync.dma_start(
+            (nc.sync, nc.scalar)[q % 2].dma_start(
                 out=plane[32 * q : 32 * q + 4, :].bitcast(I32),
                 in_=tab_scales[0][4 * q : 4 * q + 4, :].bitcast(I32),
             )
@@ -79,6 +78,7 @@ def tile_attend_csoftlarger_kernel(tc, tab_words, tab_scales, w1, gain, steep, w
             in_=tab_words[0].rearrange("p n t -> p (n t)").bitcast(I32),
         )
         nc.sync.dma_start(out=gain_sb[:], in_=gain)
+        nc.sync.dma_start(out=wo_raw[:], in_=rows_by_four(wo))
         nc.sync.dma_start(out=dy_raw[:], in_=rows_by_four(dy))
         nc.sync.dma_start(out=steep_sb[:], in_=steep)
         nc.sync.dma_start(picks3[:], offs3)
@@ -98,14 +98,13 @@ def tile_attend_csoftlarger_kernel(tc, tab_words, tab_scales, w1, gain, steep, w
         tab_bytes = sb.tile([P, J], U8, name="tab_bytes", align_bytes=64)
         nc.vector.tensor_copy(tab_bytes[:], plane[:].indirect(slots[:]))
         w1_codes, w1_scales = quantize(nc, sb, w1_grouped, "w1")
-        wo_codes, wo_scales = quantize(nc, sb, wo_grouped, "wo")
 
         half_steep = sb.tile([P, 1], F32, name="half_steep")
         nc.gpsimd.tensor_scalar(half_steep[:], steep_sb[:], 0.5, 0.0, ALU.mult, ALU.add)
         neg_half_gain = sb.tile([P, 1], F32, name="neg_half_gain")
         nc.gpsimd.tensor_scalar(neg_half_gain[:], gain_sb[:], -0.5, 0.0, ALU.mult, ALU.add)
 
-        h1 = sb.tile([P, J], F32, name="h1")
+        h1 = sb.tile([P, J], F32, name="h1", tag="wo_raw")
         j0 = 0
         for i, n in enumerate(SLOT_PIECES):
             tab_codes = sb.tile([P, n], U32, name="tab_codes%d" % i, align_bytes=64)
@@ -123,6 +122,7 @@ def tile_attend_csoftlarger_kernel(tc, tab_words, tab_scales, w1, gain, steep, w
             nc.scalar.activation(out=h1[:, j0 : j0 + n], in_=a[:], func=ACT.Copy, scale=gain_sb[:])
             j0 = j0 + n
 
+        wo_codes, wo_scales = quantize(nc, sb, wo_grouped, "wo")
         dy_grouped = sb.tile([P, M, PACK], BF16, name="dy_grouped", align_bytes=64)
         nc.vector.tensor_copy(weave_out(dy_grouped), weave_in(dy_raw))
         dy_codes, dy_scales = quantize(nc, sb, dy_grouped, "dy")
@@ -136,6 +136,7 @@ def tile_attend_csoftlarger_kernel(tc, tab_words, tab_scales, w1, gain, steep, w
             start=True,
             stop=True,
         )
+
 
         halves = [slice(h * HALF, (h + 1) * HALF) for h in range(2)]
         lists2 = [picks2[:, h * HALF // GROUP : (h + 1) * HALF // GROUP] for h in range(2)]

from contextlib import ExitStack

import concourse.mybir as mybir

K, R, F, T, J, M = 512, 128, 512, 2048, 512, 256
FLOPS = 2 * K * R * J + 2 * F * R * M

F32 = mybir.dt.float32
BF16 = mybir.dt.bfloat16
I32 = mybir.dt.int32
U32 = mybir.dt.uint32
U16 = mybir.dt.uint16
U8 = mybir.dt.uint8
FP8X4 = mybir.dt.float8_e4m3fn_x4
ALU = mybir.AluOpType
ACT = mybir.ActivationFunctionType

P = 128
PACK = 4
GROUP = 16
SLOT_PIECES = (256, 128, 128)
HALF = M // 2


def rows_by_four(x):
    return x.rearrange("(p t) w -> p t w", t=PACK)


def weave_out(grouped):
    return grouped[:].rearrange("p (c i) t -> p c t i", i=PACK)


def weave_in(raw):
    return raw[:].rearrange("p t (c i) -> p c t i", i=PACK)


def quantize(nc, pool, grouped, name):
    width = grouped.shape[1]
    codes = pool.tile([P, width], U32, name=name + "_codes", align_bytes=64)
    scales = pool.tile([P, width], U8, name=name + "_scales", align_bytes=64)
    nc.vector.quantize_mx(
        out=codes[:].bitcast(FP8X4),
        scales=scales[:],
        in_=grouped[:].rearrange("p w t -> p (w t)"),
    )
    return codes, scales


def tile_attend_csoftlarger_kernel(tc, tab_words, tab_scales, w1, gain, steep, wo, dy, old, offs, offs2, offs3, out):
    nc = tc.nc
    with ExitStack() as ctx:
        sb = ctx.enter_context(tc.tile_pool(name="sb", bufs=1))
        ps = ctx.enter_context(tc.psum_pool(name="ps", bufs=1))

        slots = sb.tile([P, J // GROUP], U16, name="slots")
        picks2 = sb.tile([P, M // GROUP], U16, name="picks2")
        picks3 = sb.tile([P, M // GROUP], U16, name="picks3")
        words = sb.tile([P, T], U32, name="words")
        plane = sb.tile([P, T], U8, name="plane")
        w1_raw = sb.tile([P, PACK, R], F32, name="w1_raw")
        wo_raw = sb.tile([P, PACK, R], F32, name="wo_raw", tag="wo_raw")
        dy_raw = sb.tile([P, PACK, M], F32, name="dy_raw")
        old_sb = sb.tile([P, J], F32, name="old_sb")
        gain_sb = sb.tile([P, 1], F32, name="gain_sb")
        steep_sb = sb.tile([P, 1], F32, name="steep_sb")

        nc.vector.memset(plane[:, : T // 2].bitcast(I32), 0)
        nc.gpsimd.memset(plane[:, T // 2 :].bitcast(I32), 0)
        nc.sync.dma_start(slots[:], offs)
        nc.sync.dma_start(out=w1_raw[:], in_=rows_by_four(w1))
        for q in range(4):
            (nc.sync, nc.scalar)[q % 2].dma_start(
                out=plane[32 * q : 32 * q + 4, :].bitcast(I32),
                in_=tab_scales[0][4 * q : 4 * q + 4, :].bitcast(I32),
            )
        nc.sync.dma_start(
            out=words[:].bitcast(I32),
            in_=tab_words[0].rearrange("p n t -> p (n t)").bitcast(I32),
        )
        nc.sync.dma_start(out=gain_sb[:], in_=gain)
        nc.sync.dma_start(out=wo_raw[:], in_=rows_by_four(wo))
        nc.sync.dma_start(out=dy_raw[:], in_=rows_by_four(dy))
        nc.sync.dma_start(out=steep_sb[:], in_=steep)
        nc.sync.dma_start(picks3[:], offs3)
        nc.sync.dma_start(picks2[:], offs2)
        nc.sync.dma_start(out=old_sb[:], in_=old)

        placed2 = sb.tile([P, J], F32, name="placed2")
        placed3 = sb.tile([P, J], F32, name="placed3")
        nc.vector.memset(placed2[:], 0.0)
        nc.vector.memset(placed3[:], 0.0)

        w1_grouped = sb.tile([P, R, PACK], BF16, name="w1_grouped", align_bytes=64)
        nc.scalar.activation(out=weave_out(w1_grouped), in_=weave_in(w1_raw), func=ACT.Copy)
        wo_grouped = sb.tile([P, R, PACK], BF16, name="wo_grouped", align_bytes=64)
        nc.scalar.activation(out=weave_out(wo_grouped), in_=weave_in(wo_raw), func=ACT.Copy)

        tab_bytes = sb.tile([P, J], U8, name="tab_bytes", align_bytes=64)
        nc.vector.tensor_copy(tab_bytes[:], plane[:].indirect(slots[:]))
        w1_codes, w1_scales = quantize(nc, sb, w1_grouped, "w1")

        half_steep = sb.tile([P, 1], F32, name="half_steep")
        nc.gpsimd.tensor_scalar(half_steep[:], steep_sb[:], 0.5, 0.0, ALU.mult, ALU.add)
        neg_half_gain = sb.tile([P, 1], F32, name="neg_half_gain")
        nc.gpsimd.tensor_scalar(neg_half_gain[:], gain_sb[:], -0.5, 0.0, ALU.mult, ALU.add)

        h1 = sb.tile([P, J], F32, name="h1", tag="wo_raw")
        j0 = 0
        for i, n in enumerate(SLOT_PIECES):
            tab_codes = sb.tile([P, n], U32, name="tab_codes%d" % i, align_bytes=64)
            nc.vector.tensor_copy(tab_codes[:], words[:].indirect(slots[:, j0 // GROUP : (j0 + n) // GROUP]))
            a = ps.tile([P, n], F32, name="a%d" % i)
            nc.tensor.matmul_mx(
                out=a[:],
                lhsT=w1_codes[:].bitcast(FP8X4),
                lhsT_scale=w1_scales[:],
                rhs=tab_codes[:].bitcast(FP8X4),
                rhs_scale=tab_bytes[:, j0 : j0 + n],
                start=True,
                stop=True,
            )
            nc.scalar.activation(out=h1[:, j0 : j0 + n], in_=a[:], func=ACT.Copy, scale=gain_sb[:])
            j0 = j0 + n

        wo_codes, wo_scales = quantize(nc, sb, wo_grouped, "wo")
        dy_grouped = sb.tile([P, M, PACK], BF16, name="dy_grouped", align_bytes=64)
        nc.vector.tensor_copy(weave_out(dy_grouped), weave_in(dy_raw))
        dy_codes, dy_scales = quantize(nc, sb, dy_grouped, "dy")
        c0 = ps.tile([P, M], F32, name="c0")
        nc.tensor.matmul_mx(
            out=c0[:],
            lhsT=wo_codes[:].bitcast(FP8X4),
            lhsT_scale=wo_scales[:],
            rhs=dy_codes[:].bitcast(FP8X4),
            rhs_scale=dy_scales[:],
            start=True,
            stop=True,
        )


        halves = [slice(h * HALF, (h + 1) * HALF) for h in range(2)]
        lists2 = [picks2[:, h * HALF // GROUP : (h + 1) * HALF // GROUP] for h in range(2)]
        lists3 = [picks3[:, h * HALF // GROUP : (h + 1) * HALF // GROUP] for h in range(2)]

        def halves_tile(name):
            return [sb.tile([P, HALF], F32, name="%s%d" % (name, h)) for h in range(2)]

        pick2 = sb.tile([P, M], F32, name="pick2", tag="pick2")
        pick3 = halves_tile("pick3")
        diff = halves_tile("diff")
        th = halves_tile("th")
        hz = halves_tile("hz")
        th_plus = halves_tile("th_plus")
        bend = halves_tile("bend")
        share = sb.tile([P, M], F32, name="share")

        nc.vector.tensor_copy(pick2[:], h1[:].indirect(picks2[:]))
        for h in range(2):
            nc.scalar.activation(out=pick3[h][:], in_=h1[:].indirect(lists3[h]), func=ACT.Copy)
        for h in range(2):
            nc.vector.tensor_tensor(diff[h][:], pick2[:, halves[h]], pick3[h][:], ALU.subtract)
            nc.scalar.activation(out=th[h][:], in_=diff[h][:], func=ACT.Tanh, scale=half_steep[:])
            nc.scalar.activation(out=th_plus[h][:], in_=th[h][:], func=ACT.Copy, bias=1.0)
        for h in range(2):
            nc.vector.tensor_scalar(hz[h][:], diff[h][:], half_steep[:], None, ALU.mult)
        grad = sb.tile([P, M], F32, name="grad", tag="pick2")
        nc.scalar.activation(out=grad[:], in_=c0[:], func=ACT.Copy, scale=neg_half_gain[:])
        for h in range(2):
            nc.vector.scalar_tensor_tensor(bend[h][:], th[h][:], 1.0, hz[h][:], ALU.subtract, ALU.mult)
        for h in range(2):
            nc.vector.scalar_tensor_tensor(share[:, halves[h]], bend[h][:], 1.0, th_plus[h][:], ALU.subtract, ALU.mult)
        neg_sent3 = sb.tile([P, M], F32, name="neg_sent3")
        nc.vector.tensor_tensor(placed2[:].indirect(lists2[0]), grad[:, halves[0]], share[:, halves[0]], ALU.mult)
        nc.vector.scalar_tensor_tensor(neg_sent3[:], share[:], 2.0, grad[:], ALU.add, ALU.mult)
        nc.vector.tensor_tensor(placed2[:].indirect(lists2[1]), grad[:, halves[1]], share[:, halves[1]], ALU.mult)
        nc.vector.tensor_copy(placed3[:].indirect(picks3[:]), neg_sent3[:])

        columns = [slice(h * J // 2, (h + 1) * J // 2) for h in range(2)]
        partial = [sb.tile([P, J // 2], F32, name="partial%d" % h) for h in range(2)]
        for h in range(2):
            nc.gpsimd.tensor_tensor(partial[h][:], placed2[:, columns[h]], old_sb[:, columns[h]], ALU.add)
        for h in range(2):
            result = sb.tile([P, J // 2], F32, name="result%d" % h)
            nc.vector.tensor_tensor(result[:], partial[h][:], placed3[:, columns[h]], ALU.subtract)
            (nc.sync, nc.scalar)[h].dma_start(out=out[:, columns[h]], in_=result[:])
